import numpy as np
import ml_dtypes


def mxq(x, axis, fmt="e4m3"):
    dtype, down = {"e4m3": (ml_dtypes.float8_e4m3fn, 7), "e5m2": (ml_dtypes.float8_e5m2, 14)}[fmt]
    v = np.moveaxis(np.asarray(x, np.float32).astype(ml_dtypes.bfloat16).astype(np.float64), axis, -1)
    blocks = v.reshape(v.shape[:-1] + (-1, 32))
    amax = np.abs(blocks).max(-1, keepdims=True)
    byte = np.maximum(np.where(amax > 0, np.frexp(amax)[1] - 1 + 127, 0) - down, 1)
    scale = np.exp2(byte - 127.0)
    codes = (blocks / scale).astype(np.float32).astype(dtype).astype(np.float64)
    return np.moveaxis((codes * scale).reshape(v.shape), -1, axis)


WIDE = False


def mx_kscale(k):
    if not WIDE:
        return np.ones(k)
    levels = np.array([10, -10, 5, -5, 0])
    if k % 512:
        return np.exp2(np.random.permutation(np.resize(levels, k // 32))).repeat(32)
    a = np.empty((k // 512, 16))
    for p in range(k // 512):
        a[p, :8] = np.random.permutation(np.resize(levels, 8))
        for g in range(8):
            far = levels[np.abs(levels - a[p, g]) >= 10]
            a[p, g + 8] = far[np.random.randint(len(far))]
    return np.exp2(a.ravel()).repeat(32)


def f64(x):
    return np.asarray(x).astype(np.float64)


def striped(idx):
    return np.tile(idx.reshape(-1, 16).T, (8, 1)).astype(np.uint16)


def unstriped(offs):
    return offs[:16].T.reshape(-1).astype(np.int64)


E2M1 = np.array([0.0, 0.5, 1.0, 1.5, 2.0, 3.0, 4.0, 6.0, -0.0, -0.5, -1.0, -1.5, -2.0, -3.0, -4.0, -6.0])


def pack_weight(w, fmt):
    k, n = w.shape
    w = f64(np.asarray(w, np.float32).astype(ml_dtypes.bfloat16)).reshape(k // 32, 32, n)
    amax = np.abs(w).max(1)
    if fmt == "e4m3":
        byte = np.frexp(amax)[1] - 1 + 127 - 7
    else:
        mant, ex = np.frexp(amax / 6.0)
        byte = np.where(mant > 0.5, ex, ex - 1) + 127
    byte = np.clip(np.where(amax > 0, byte, 1), 1, 254)
    scaled = (w * np.exp2(127.0 - byte)[:, None, :]).reshape(k, n).astype(np.float32)
    by_word = np.ascontiguousarray(scaled.reshape(k // 512, 128, 4, n).transpose(0, 1, 3, 2))
    if fmt == "e4m3":
        words = by_word.astype(ml_dtypes.float8_e4m3fn).view(np.uint8)
    else:
        c = by_word.astype(ml_dtypes.float4_e2m1fn).view(np.uint8) & 0xF
        words = (c[..., 0::2] | (c[..., 1::2] << 4)).reshape(k // 512, 128, 2 * n)
    return np.ascontiguousarray(words), np.ascontiguousarray(byte.astype(np.uint8).reshape(k // 512, 16, n))


def unpack_weight(words, scales, fmt):
    g, _, n = scales.shape
    words = np.ascontiguousarray(words).reshape(g, 128, n, -1)
    if fmt == "e4m3":
        vals = words.view(ml_dtypes.float8_e4m3fn).astype(np.float64)
    else:
        nib = np.empty((g, 128, n, 4), np.uint8)
        nib[..., 0::2] = words & 0xF
        nib[..., 1::2] = words >> 4
        vals = E2M1[nib]
    vals = vals * np.repeat(np.exp2(scales.astype(np.float64) - 127.0), 8, axis=1)[..., None]
    return vals.transpose(0, 1, 3, 2).reshape(g * 512, n)


def gelu(v):
    return 0.5 * v * (1.0 + np.tanh(np.sqrt(2.0 / np.pi) * (v + 0.044715 * v**3)))


T, S, T3, P, K, K2, H, N = 4096, 1024, 2048, 512, 1024, 512, 1024, 256


def setup_inputs():
    n = np.random.standard_normal
    s, s2, u = mx_kscale(K)[:, None], mx_kscale(K2)[:, None], mx_kscale(H)[:, None]
    d = {}
    d["tab_words"], d["tab_scales"] = pack_weight(n((K, T)) * s, "e4m3")
    d["tab2_words"], d["tab2_scales"] = pack_weight(n((K2, T3)) * s2, "e4m3")
    d["offs"] = striped(np.random.permutation(T)[:S])
    d["offs2"] = striped(np.random.permutation(T3)[:P])
    d["pos1"] = striped(np.random.permutation(S)[:P])
    d["w1"] = (2.5 * n((K, H)) / s / K ** 0.5).astype(np.float32)
    d["w2_words"], d["w2_scales"] = pack_weight(1.2 * n((K2, H)) / s2 * u.T / K2 ** 0.5, "e4m3")
    d["w3_words"], d["w3_scales"] = pack_weight(2.0 * n((K2, H)) / s2 / K2 ** 0.5, "e2m1")
    d["w4"] = (1.5 * n((H, N)) / u / H ** 0.5).astype(np.float32)
    d["brief"] = (1.4 * n((H, S)) * u).astype(np.float32)
    d["gain"] = (np.exp(0.3 * n(H)) * u[:, 0]).astype(np.float32)
    d["wgs"] = np.exp(0.3 * n((128, P))).astype(np.float32)
    return d


def reference(tab_words, tab_scales, tab2_words, tab2_scales, offs, offs2, pos1, w1,
              w2_words, w2_scales, w3_words, w3_scales, w4, brief, gain, wgs):
    v = unpack_weight(tab_words, tab_scales, "e4m3")[:, unstriped(offs)]
    v2 = unpack_weight(tab2_words, tab2_scales, "e4m3")[:, unstriped(offs2)]
    w2 = unpack_weight(w2_words, w2_scales, "e4m3")
    w3 = unpack_weight(w3_words, w3_scales, "e2m1")
    e = mxq(f64(w1), 0, "e4m3").T @ v
    a = f64(brief) / (1.0 + np.exp(-e))
    b = (w2.T @ v2) - f64(gain)[:, None] * np.tanh(w3.T @ v2)
    placed = np.zeros((H, S))
    placed[:, unstriped(pos1)] = np.tile(f64(wgs), (H // 128, 1)) * b
    z = np.maximum(a, placed)
    out = mxq(f64(w4), 0, "e4m3").T @ mxq(z, 0, "e4m3")
    return out

@@ -1,0 +1,248 @@
+from contextlib import ExitStack
+
+import concourse.mybir as mybir
+
+F32 = mybir.dt.float32
+BF16 = mybir.dt.bfloat16
+I32 = mybir.dt.int32
+U32 = mybir.dt.uint32
+U16 = mybir.dt.uint16
+U8 = mybir.dt.uint8
+FP8X4 = mybir.dt.float8_e4m3fn_x4
+FP4X4 = mybir.dt.float4_e2m1fn_x4
+ALU = mybir.AluOpType
+ACT = mybir.ActivationFunctionType
+
+T, S, T2, M, K, K2, H, N = 4096, 1024, 2048, 512, 1024, 512, 1024, 256
+FLOPS = 2 * K * H * S + 2 * 2 * K2 * H * M + 2 * H * N * S
+P = 128
+BANK = 512
+CHUNK = 256
+
+
+def tile_list_accord_slot_max_kernel(tc, tab_words, tab_scales, tab2_words, tab2_scales, offs, offs2, pos1, w1,
+                                              w2_words, w2_scales, w3_words, w3_scales, w4, brief, gain, wgs, out):
+    nc = tc.nc
+    with ExitStack() as ctx:
+        lists = ctx.enter_context(tc.tile_pool(name="lists", bufs=1))
+        sb = ctx.enter_context(tc.tile_pool(name="sb", bufs=1))
+        ps = ctx.enter_context(tc.psum_pool(name="ps", bufs=2))
+
+        def tile(shape, dtype, name, tag=None, bufs=1):
+            return sb.tile(shape, dtype, name=name, tag=tag or name, bufs=bufs, align_bytes=64)
+
+        idx = lists.tile([P, S // 16], U16, name="idx")
+        idx2 = lists.tile([P, M // 16], U16, name="idx2")
+        slot = lists.tile([P, M // 16], U16, name="slot")
+
+        tab2_s = tile([P, T2], U8, "tab2_s")
+        w23_s = tile([P, H], U8, "w23_s")
+        tab_s = tile([P, T], U8, "tab_s")
+        pages = [tile([P, S], F32, "page%d" % i) for i in range(2)]
+        nc.vector.memset(tab2_s[:].bitcast(I32), 0)
+        nc.vector.memset(w23_s[:].bitcast(I32), 0)
+        nc.vector.memset(tab_s[:].bitcast(I32), 0)
+        for page in pages:
+            nc.vector.memset(page[:], 0.0)
+
+        w2_raw = tile([P, H], I32, "w2_raw")
+        w3_raw = tile([P, H], U16, "w3_raw")
+        tab2_w = tile([P, T2], I32, "tab2_w", tag="tab2_w4")
+        tab_w = [tile([P, T], I32, "tab_w%d" % a, tag="big%d" % a) for a in range(2)]
+        gain_t = tile([P, 2, 4], F32, "gain_t")
+        wgs_t = tile([P, 4, M], F32, "wgs_t")
+
+        def words(src):
+            return src.rearrange("p c i -> p (c i)").bitcast(I32)
+
+        def load_scales(queue, plane, first, src):
+            for q in range(4):
+                queue.dma_start(out=plane[32 * q + first : 32 * q + first + 4, :].bitcast(I32), in_=src[4 * q : 4 * q + 4, :].bitcast(I32))
+
+        load_scales(nc.sync, tab2_s, 0, tab2_scales[0])
+        nc.sync.dma_start(idx2[:], offs2)
+        nc.sync.dma_start(out=tab2_w[:], in_=words(tab2_words[0]))
+        nc.sync.dma_start(out=w2_raw[:], in_=words(w2_words[0]))
+        nc.sync.dma_start(out=w3_raw[:].bitcast(I32), in_=w3_words[0].bitcast(I32))
+        load_scales(nc.sync, w23_s, 0, w3_scales[0])
+        load_scales(nc.sync, w23_s, 4, w2_scales[0])
+        nc.sync.dma_start(out=tab_w[0][:, : T // 2], in_=words(tab_words[0])[:, : T // 2])
+        load_scales(nc.sync, tab_s, 0, tab_scales[0])
+        nc.sync.dma_start(idx[:], offs)
+        nc.sync.dma_start(out=gain_t[:], in_=gain.rearrange("(b p t) -> p b t", b=2, t=4))
+        nc.sync.dma_start(out=tab_w[0][:, T // 2 :], in_=words(tab_words[0])[:, T // 2 :])
+        load_scales(nc.sync, tab_s, 4, tab_scales[1])
+        nc.sync.dma_start(slot[:], pos1)
+        nc.sync.dma_start(out=tab_w[1][:], in_=words(tab_words[1]))
+        for q in range(4):
+            nc.sync.dma_start(out=wgs_t[32 * q : 32 * q + 32, :, :], in_=wgs.rearrange("(p t) m -> p t m", t=4))
+
+        def load_w1(b, a, dst):
+            nc.sync.dma_start(out=dst, in_=w1[512 * a : 512 * a + 512, 512 * b : 512 * b + 512].rearrange("(p j) c -> p j c", j=4))
+
+        def load_brief(b, t, dst):
+            nc.sync.dma_start(out=dst, in_=brief[512 * b : 512 * b + 512, :].rearrange("(p t) j -> p t j", t=4)[:, t, :])
+
+        w1_raw = {}
+        brief_t = {}
+        for a in range(2):
+            raw = tile([P, 4, 512], F32, "w1_raw0%d" % a)
+            load_w1(0, a, raw[:])
+            w1_raw[0, a] = raw[:]
+
+        def load_brief_lo(t):
+            rows = tile([P, S], F32, "brief0%d" % t)
+            load_brief(0, t, rows[:])
+            brief_t[t] = rows[:]
+
+        load_brief_lo(0)
+        load_brief_lo(1)
+
+        w2_c = tile([P, H], I32, "w2_c")
+        w3_c = tile([P, H], U16, "w3_c")
+        w23_cs = tile([P, H], U8, "w23_cs")
+
+        def deal(dst, src, run):
+            nc.vector.tensor_copy(out=dst[:].rearrange("p (b t m i) -> p b m t i", b=2, t=4, i=run),
+                                  in_=src[:].rearrange("p (b m i t) -> p b m t i", b=2, t=4, i=run))
+
+        deal(w2_c, w2_raw, 4)
+        deal(w3_c, w3_raw, 8)
+        deal(w23_cs, w23_s, 16)
+
+        v2_w = tile([P, M], U32, "v2_w")
+        v2_s = tile([P, M], U8, "v2_s")
+        nc.vector.tensor_copy(v2_w[:], tab2_w[:].bitcast(U32).indirect(idx2[:]))
+        nc.vector.tensor_copy(v2_s[:], tab2_s[:].indirect(idx2[:]))
+
+        b_t = []
+        for s in range(8):
+            cols = slice(P * s, P * s + P)
+            lin = ps.tile([P, M], F32, name="lin", tag="lin")
+            arg = ps.tile([P, M], F32, name="arg", tag="arg")
+            nc.tensor.matmul_mx(out=arg[:], lhsT=w3_c[:, cols].bitcast(FP4X4), lhsT_scale=w23_cs[:, cols],
+                                rhs=v2_w[:].bitcast(FP8X4), rhs_scale=v2_s[:], start=True, stop=True)
+            nc.tensor.matmul_mx(out=lin[:], lhsT=w2_c[:, cols].bitcast(FP8X4), lhsT_scale=w23_cs[4:P, cols],
+                                rhs=v2_w[:].bitcast(FP8X4), rhs_scale=v2_s[:], start=True, stop=True)
+            th = tile([P, M], F32, "th", bufs=2)
+            nc.scalar.activation(out=th[:], in_=arg[:], func=ACT.Tanh, scale=-1.0)
+            b = tile([P, M], F32, "b%d" % s)
+            nc.vector.scalar_tensor_tensor(out=b[:], in0=th[:], scalar=gain_t[:, s // 4, s % 4 : s % 4 + 1], in1=lin[:],
+                                           op0=ALU.mult, op1=ALU.add)
+            b_t.append(b)
+
+        v_w = [tile([P, S], U32, "v_w%d" % a) for a in range(2)]
+        v_s = tile([P, S], U8, "v_s")
+        nc.vector.tensor_copy(v_w[0][:], tab_w[0][:].bitcast(U32).indirect(idx[:]))
+        nc.vector.tensor_copy(v_s[:], tab_s[:].indirect(idx[:]))
+        nc.vector.tensor_copy(v_w[1][:], tab_w[1][:].bitcast(U32).indirect(idx[:]))
+
+        w1_hi = tile([P, 2, 4, 512], F32, "w1_hi", tag="big0")
+        for a in range(2):
+            load_w1(1, a, w1_hi[:, a])
+            w1_raw[1, a] = w1_hi[:, a]
+        load_brief_lo(2)
+        load_brief_lo(3)
+        brief_hi = tile([P, 4, S], F32, "brief_hi", tag="big1")
+        for t in range(4):
+            load_brief(1, t, brief_hi[:, t, :])
+            brief_t[4 + t] = brief_hi[:, t, :]
+        w4_raw = tile([P, 2, 4, N], F32, "w4_raw", tag="tab2_w4")
+        nc.sync.dma_start(out=w4_raw[:], in_=w4.rearrange("(b p j) n -> p b j n", b=2, j=4))
+
+        w1_c = {}
+        w1_s = {}
+
+        def quantise_w1(b):
+            for a in range(2):
+                rounded = tile([P, 2048], BF16, "w1_bf%d%d" % (b, a), tag="w1_bf%d%d" % (b, a))
+                dst = rounded[:].rearrange("p (t m j) -> p m t j", t=4, j=4)
+                src = w1_raw[b, a].rearrange("p j (m t) -> p m t j", t=4)
+                for h in range(2):
+                    nc.scalar.copy(out=dst[:, 64 * h : 64 * h + 64], in_=src[:, 64 * h : 64 * h + 64])
+                w1_c[b, a] = tile([P, 512], U32, "w1_c%d%d" % (b, a))
+                w1_s[b, a] = tile([P, 512], U8, "w1_s%d%d" % (b, a))
+                nc.vector.quantize_mx(out=w1_c[b, a][:].bitcast(FP8X4), scales=w1_s[b, a][:], in_=rounded[:])
+
+        quantise_w1(0)
+
+        wb_first = tile([P, 2, M], F32, "wb_first", tag="w1_bf01")
+        wb = []
+        for s in range(8):
+            dst = wb_first[:, s, :] if s < 2 else b_t[s][:]
+            nc.gpsimd.tensor_tensor(out=dst, in0=b_t[s][:], in1=wgs_t[:, s % 4, :], op=ALU.mult)
+            wb.append(dst)
+
+        a_t = {}
+
+        def front(s):
+            b, t = divmod(s, 4)
+            nc.vector.tensor_copy(pages[s % 2][:].indirect(slot[:]), wb[s])
+            sig = tile([P, S], F32, "sig", bufs=3)
+            cols = slice(P * t, P * t + P)
+            for h in range(2):
+                e = ps.tile([P, BANK], F32, name="e", tag="e", bufs=4)
+                js = slice(BANK * h, BANK * h + BANK)
+                for a in range(2):
+                    nc.tensor.matmul_mx(out=e[:], lhsT=w1_c[b, a][:, cols].bitcast(FP8X4), lhsT_scale=w1_s[b, a][:, cols],
+                                        rhs=v_w[a][:, js].bitcast(FP8X4), rhs_scale=v_s[4 * a : P, js], start=(a == 0), stop=(a == 1))
+                nc.scalar.activation(out=sig[:, js], in_=e[:], func=ACT.Sigmoid)
+            a_t[s] = tile([P, S], F32, "a", bufs=2)
+            nc.gpsimd.tensor_tensor(out=a_t[s][:], in0=brief_t[s], in1=sig[:], op=ALU.mult)
+
+        z_lo = tile([P, 4, S], BF16, "z_lo")
+        z_hi = [tile([P, 4, CHUNK], BF16, "z_hi%d" % c) for c in range(4)]
+
+        def larger(s):
+            b, t = divmod(s, 4)
+            if b == 0:
+                nc.vector.tensor_tensor(out=z_lo[:, t, :], in0=a_t[s][:], in1=pages[s % 2][:], op=ALU.max)
+            else:
+                for c in range(4):
+                    js = slice(CHUNK * c, CHUNK * c + CHUNK)
+                    nc.vector.tensor_tensor(out=z_hi[c][:, t, :], in0=a_t[s][:, js], in1=pages[s % 2][:, js], op=ALU.max)
+
+        front(0)
+        front(1)
+        for s in range(8):
+            larger(s)
+            if s + 2 == 4:
+                quantise_w1(1)
+            if s + 2 < 8:
+                front(s + 2)
+
+        z_c = {}
+        z_s = {}
+
+        def quantise_z(b, c, src, copy):
+            woven = tile([P, 4 * CHUNK], BF16, "woven", bufs=4)
+            copy(out=woven[:].rearrange("p (c i t) -> p c t i", i=4, t=4), in_=src.rearrange("p t (c i) -> p c t i", i=4))
+            z_c[b, c] = tile([P, CHUNK], U32, "z_c%d%d" % (b, c))
+            z_s[b, c] = tile([P, CHUNK], U8, "z_s%d%d" % (b, c))
+            nc.vector.quantize_mx(out=z_c[b, c][:].bitcast(FP8X4), scales=z_s[b, c][:], in_=woven[:])
+
+        for c in range(4):
+            quantise_z(0, c, z_lo[:, :, CHUNK * c : CHUNK * c + CHUNK], nc.scalar.copy)
+
+        w4_bf = tile([P, 2, 4 * N], BF16, "w4_bf")
+        for b in range(2):
+            nc.scalar.copy(out=w4_bf[:, b, :].rearrange("p (c i j) -> p c j i", i=4, j=4), in_=w4_raw[:, b].rearrange("p j (c i) -> p c j i", i=4))
+        w4_c = tile([P, 2 * N], U32, "w4_c")
+        w4_s = tile([P, 2 * N], U8, "w4_s")
+        nc.vector.quantize_mx(out=w4_c[:].bitcast(FP8X4), scales=w4_s[:], in_=w4_bf[:].rearrange("p b x -> p (b x)"))
+
+        for c in range(4):
+            quantise_z(1, c, z_hi[c][:], nc.scalar.copy if c < 2 else nc.vector.tensor_copy)
+        for c in range(4):
+            acc = ps.tile([P, 2, CHUNK], F32, name="acc", tag="lin" if c % 2 == 0 else "arg")
+            for n in range(2):
+                for b in range(2):
+                    cols = slice(N * b + P * n, N * b + P * n + P)
+                    nc.tensor.matmul_mx(out=acc[:, n, :], lhsT=w4_c[:, cols].bitcast(FP8X4), lhsT_scale=w4_s[:, cols],
+                                        rhs=z_c[b, c][:].bitcast(FP8X4), rhs_scale=z_s[b, c][:], start=(b == 0), stop=(b == 1))
+            res = tile([P, 2, CHUNK], F32, "res", bufs=4)
+            if c % 2 == 0:
+                nc.scalar.copy(out=res[:], in_=acc[:])
+            else:
+                nc.vector.tensor_copy(out=res[:], in_=acc[:])
+            nc.sync.dma_start(out=out[:, CHUNK * c : CHUNK * c + CHUNK].rearrange("(n p) j -> p n j", n=2), in_=res[:])

@@ -67,15 +67,16 @@ def tile_list_accord_slot_max_kernel(tc, tab_words, tab_scales, tab2_words, tab2
         load_scales(nc.sync, w23_s, 0, w3_scales[0])
         load_scales(nc.sync, w23_s, 4, w2_scales[0])
         nc.sync.dma_start(out=tab_w[0][:, : T // 2], in_=words(tab_words[0])[:, : T // 2])
-        load_scales(nc.sync, tab_s, 0, tab_scales[0])
-        nc.sync.dma_start(idx[:], offs)
         nc.sync.dma_start(out=gain_t[:], in_=gain.rearrange("(b p t) -> p b t", b=2, t=4))
-        nc.sync.dma_start(out=tab_w[0][:, T // 2 :], in_=words(tab_words[0])[:, T // 2 :])
-        load_scales(nc.sync, tab_s, 4, tab_scales[1])
         nc.sync.dma_start(slot[:], pos1)
-        nc.sync.dma_start(out=tab_w[1][:], in_=words(tab_words[1]))
         for q in range(4):
             nc.sync.dma_start(out=wgs_t[32 * q : 32 * q + 32, :, :], in_=wgs.rearrange("(p t) m -> p t m", t=4))
+        nc.sync.dma_start(idx[:], offs)
+        nc.sync.dma_start(out=tab_w[0][:, T // 2 :], in_=words(tab_words[0])[:, T // 2 :])
+        load_scales(nc.sync, tab_s, 0, tab_scales[0])
+        nc.sync.dma_start(out=tab_w[1][:, : T // 2], in_=words(tab_words[1])[:, : T // 2])
+        load_scales(nc.sync, tab_s, 4, tab_scales[1])
+        nc.sync.dma_start(out=tab_w[1][:, T // 2 :], in_=words(tab_words[1])[:, T // 2 :])
 
         def load_w1(b, a, dst):
             nc.sync.dma_start(out=dst, in_=w1[512 * a : 512 * a + 512, 512 * b : 512 * b + 512].rearrange("(p j) c -> p j c", j=4))
@@ -115,8 +116,9 @@ def tile_list_accord_slot_max_kernel(tc, tab_words, tab_scales, tab2_words, tab2
         nc.vector.tensor_copy(v2_w[:], tab2_w[:].bitcast(U32).indirect(idx2[:]))
         nc.vector.tensor_copy(v2_s[:], tab2_s[:].indirect(idx2[:]))
 
-        b_t = []
-        for s in range(8):
+        b_t = {}
+
+        def accord(s):
             cols = slice(P * s, P * s + P)
             lin = ps.tile([P, M], F32, name="lin", tag="lin")
             arg = ps.tile([P, M], F32, name="arg", tag="arg")
@@ -126,10 +128,13 @@ def tile_list_accord_slot_max_kernel(tc, tab_words, tab_scales, tab2_words, tab2
                                 rhs=v2_w[:].bitcast(FP8X4), rhs_scale=v2_s[:], start=True, stop=True)
             th = tile([P, M], F32, "th", bufs=2)
             nc.scalar.activation(out=th[:], in_=arg[:], func=ACT.Tanh, scale=-1.0)
-            b = tile([P, M], F32, "b%d" % s)
+            b = tile([P, M], F32, "b%d" % s, tag="w1_bf01" if s == 1 else None)
             nc.vector.scalar_tensor_tensor(out=b[:], in0=th[:], scalar=gain_t[:, s // 4, s % 4 : s % 4 + 1], in1=lin[:],
                                            op0=ALU.mult, op1=ALU.add)
-            b_t.append(b)
+            b_t[s] = b
+
+        for s in (0, 2, 3, 4, 5, 6, 7):
+            accord(s)
 
         v_w = [tile([P, S], U32, "v_w%d" % a) for a in range(2)]
         v_s = tile([P, S], U8, "v_s")
@@ -143,12 +148,12 @@ def tile_list_accord_slot_max_kernel(tc, tab_words, tab_scales, tab2_words, tab2
             w1_raw[1, a] = w1_hi[:, a]
         load_brief_lo(2)
         load_brief_lo(3)
+        w4_raw = tile([P, 2, 4, N], F32, "w4_raw", tag="tab2_w4")
+        nc.sync.dma_start(out=w4_raw[:], in_=w4.rearrange("(b p j) n -> p b j n", b=2, j=4))
         brief_hi = tile([P, 4, S], F32, "brief_hi", tag="big1")
         for t in range(4):
             load_brief(1, t, brief_hi[:, t, :])
             brief_t[4 + t] = brief_hi[:, t, :]
-        w4_raw = tile([P, 2, 4, N], F32, "w4_raw", tag="tab2_w4")
-        nc.sync.dma_start(out=w4_raw[:], in_=w4.rearrange("(b p j) n -> p b j n", b=2, j=4))
 
         w1_c = {}
         w1_s = {}
@@ -166,18 +171,13 @@ def tile_list_accord_slot_max_kernel(tc, tab_words, tab_scales, tab2_words, tab2
 
         quantise_w1(0)
 
-        wb_first = tile([P, 2, M], F32, "wb_first", tag="w1_bf01")
-        wb = []
-        for s in range(8):
-            dst = wb_first[:, s, :] if s < 2 else b_t[s][:]
-            nc.gpsimd.tensor_tensor(out=dst, in0=b_t[s][:], in1=wgs_t[:, s % 4, :], op=ALU.mult)
-            wb.append(dst)
+        accord(1)
 
-        a_t = {}
+        def place(s):
+            nc.vector.tensor_tensor(pages[s % 2][:].indirect(slot[:]), b_t[s][:], wgs_t[:, s % 4, :], ALU.mult)
 
-        def front(s):
+        def gate(s):
             b, t = divmod(s, 4)
-            nc.vector.tensor_copy(pages[s % 2][:].indirect(slot[:]), wb[s])
             sig = tile([P, S], F32, "sig", bufs=3)
             cols = slice(P * t, P * t + P)
             for h in range(2):
@@ -187,8 +187,7 @@ def tile_list_accord_slot_max_kernel(tc, tab_words, tab_scales, tab2_words, tab2
                     nc.tensor.matmul_mx(out=e[:], lhsT=w1_c[b, a][:, cols].bitcast(FP8X4), lhsT_scale=w1_s[b, a][:, cols],
                                         rhs=v_w[a][:, js].bitcast(FP8X4), rhs_scale=v_s[4 * a : P, js], start=(a == 0), stop=(a == 1))
                 nc.scalar.activation(out=sig[:, js], in_=e[:], func=ACT.Sigmoid)
-            a_t[s] = tile([P, S], F32, "a", bufs=2)
-            nc.gpsimd.tensor_tensor(out=a_t[s][:], in0=brief_t[s], in1=sig[:], op=ALU.mult)
+            nc.vector.tensor_tensor(out=brief_t[s], in0=brief_t[s], in1=sig[:], op=ALU.mult)
 
         z_lo = tile([P, 4, S], BF16, "z_lo")
         z_hi = [tile([P, 4, CHUNK], BF16, "z_hi%d" % c) for c in range(4)]
@@ -196,20 +195,23 @@ def tile_list_accord_slot_max_kernel(tc, tab_words, tab_scales, tab2_words, tab2
         def larger(s):
             b, t = divmod(s, 4)
             if b == 0:
-                nc.vector.tensor_tensor(out=z_lo[:, t, :], in0=a_t[s][:], in1=pages[s % 2][:], op=ALU.max)
+                nc.vector.tensor_tensor(out=z_lo[:, t, :], in0=brief_t[s], in1=pages[s % 2][:], op=ALU.max)
             else:
                 for c in range(4):
                     js = slice(CHUNK * c, CHUNK * c + CHUNK)
-                    nc.vector.tensor_tensor(out=z_hi[c][:, t, :], in0=a_t[s][:, js], in1=pages[s % 2][:, js], op=ALU.max)
+                    nc.vector.tensor_tensor(out=z_hi[c][:, t, :], in0=brief_t[s][:, js], in1=pages[s % 2][:, js], op=ALU.max)
 
-        front(0)
-        front(1)
+        for s in range(2):
+            place(s)
+        for s in range(2):
+            gate(s)
         for s in range(8):
             larger(s)
             if s + 2 == 4:
                 quantise_w1(1)
             if s + 2 < 8:
-                front(s + 2)
+                gate(s + 2)
+                place(s + 2)
 
         z_c = {}
         z_s = {}

@@ -1,6 +1,7 @@
 from contextlib import ExitStack
 
 import concourse.mybir as mybir
+from concourse.masks import make_identity
 
 F32 = mybir.dt.float32
 BF16 = mybir.dt.bfloat16
@@ -38,51 +39,77 @@ def tile_list_accord_slot_max_kernel(tc, tab_words, tab_scales, tab2_words, tab2
         tab2_s = tile([P, T2], U8, "tab2_s")
         w23_s = tile([P, H], U8, "w23_s")
         tab_s = tile([P, T], U8, "tab_s")
-        pages = [tile([P, S], F32, "page%d" % i) for i in range(2)]
+        pages = [tile([P, S], F32, "page%d" % i) for i in range(5)]
         nc.vector.memset(tab2_s[:].bitcast(I32), 0)
         nc.vector.memset(w23_s[:].bitcast(I32), 0)
         nc.vector.memset(tab_s[:].bitcast(I32), 0)
-        for page in pages:
-            nc.vector.memset(page[:], 0.0)
 
-        w2_raw = tile([P, H], I32, "w2_raw")
+        w2_raw = tile([P, H], U32, "w2_raw")
         w3_raw = tile([P, H], U16, "w3_raw")
         tab2_w = tile([P, T2], I32, "tab2_w", tag="tab2_w4")
         tab_w = [tile([P, T], I32, "tab_w%d" % a, tag="big%d" % a) for a in range(2)]
-        gain_t = tile([P, 2, 4], F32, "gain_t")
+        gain_t = tile([P, 8], F32, "gain_t")
+        gain_rows = tile([P, P], F32, "gain_rows")
+        nc.gpsimd.memset(gain_rows[:], 0.0)
         wgs_t = tile([P, 4, M], F32, "wgs_t")
+        wgs_raw = tile([P, M], F32, "wgs_raw")
+        ident = tile([P, P], F32, "ident")
+        make_identity(nc, ident[:])
 
         def words(src):
             return src.rearrange("p c i -> p (c i)").bitcast(I32)
 
-        def load_scales(queue, plane, first, src):
-            for q in range(4):
-                queue.dma_start(out=plane[32 * q + first : 32 * q + first + 4, :].bitcast(I32), in_=src[4 * q : 4 * q + 4, :].bitcast(I32))
+        def load_scale_rows(plane, first, src, r):
+            nc.sync.dma_start(out=plane[first + r : P : 32, :].bitcast(I32), in_=src[r : 16 : 4, :].bitcast(I32))
 
-        load_scales(nc.sync, tab2_s, 0, tab2_scales[0])
+        for r in range(4):
+            load_scale_rows(tab2_s, 0, tab2_scales[0], r)
+        nc.sync.dma_start(out=wgs_raw[:], in_=wgs)
         nc.sync.dma_start(idx2[:], offs2)
         nc.sync.dma_start(out=tab2_w[:], in_=words(tab2_words[0]))
-        nc.sync.dma_start(out=w2_raw[:], in_=words(w2_words[0]))
+        nc.sync.dma_start(out=w2_raw[:].bitcast(I32), in_=words(w2_words[0]))
         nc.sync.dma_start(out=w3_raw[:].bitcast(I32), in_=w3_words[0].bitcast(I32))
-        load_scales(nc.sync, w23_s, 0, w3_scales[0])
-        load_scales(nc.sync, w23_s, 4, w2_scales[0])
-        nc.sync.dma_start(out=tab_w[0][:, : T // 2], in_=words(tab_words[0])[:, : T // 2])
-        nc.sync.dma_start(out=gain_t[:], in_=gain.rearrange("(b p t) -> p b t", b=2, t=4))
+        for r in range(4):
+            load_scale_rows(w23_s, 0, w3_scales[0], r)
+            load_scale_rows(w23_s, 4, w2_scales[0], r)
+        for b in range(2):
+            nc.sync.dma_start(out=gain_rows[4 * b : 4 * b + 4, :].rearrange("t (q i) -> t q i", i=8),
+                              in_=gain[512 * b : 512 * b + 512].rearrange("(q t i) -> t q i", t=4, i=8))
         nc.sync.dma_start(slot[:], pos1)
-        for q in range(4):
-            nc.sync.dma_start(out=wgs_t[32 * q : 32 * q + 32, :, :], in_=wgs.rearrange("(p t) m -> p t m", t=4))
         nc.sync.dma_start(idx[:], offs)
+        nc.sync.dma_start(out=tab_w[0][:, : T // 2], in_=words(tab_words[0])[:, : T // 2])
         nc.sync.dma_start(out=tab_w[0][:, T // 2 :], in_=words(tab_words[0])[:, T // 2 :])
-        load_scales(nc.sync, tab_s, 0, tab_scales[0])
+        for r in range(2):
+            for a in range(2):
+                load_scale_rows(tab_s, 4 * a, tab_scales[a], r)
         nc.sync.dma_start(out=tab_w[1][:, : T // 2], in_=words(tab_words[1])[:, : T // 2])
-        load_scales(nc.sync, tab_s, 4, tab_scales[1])
+        for r in range(2, 4):
+            for a in range(2):
+                load_scale_rows(tab_s, 4 * a, tab_scales[a], r)
         nc.sync.dma_start(out=tab_w[1][:, T // 2 :], in_=words(tab_words[1])[:, T // 2 :])
 
         def load_w1(b, a, dst):
             nc.sync.dma_start(out=dst, in_=w1[512 * a : 512 * a + 512, 512 * b : 512 * b + 512].rearrange("(p j) c -> p j c", j=4))
 
         def load_brief(b, t, dst):
-            nc.sync.dma_start(out=dst, in_=brief[512 * b : 512 * b + 512, :].rearrange("(p t) j -> p t j", t=4)[:, t, :])
+            nc.sync.dma_start(out=dst, in_=brief[512 * b : 512 * b + 512, :].rearrange("(q t i) j -> t q i j", t=4, i=8)[t])
+
+        turned = ps.tile([P, 4, P], F32, name="turned", tag="e", bufs=4)
+        for mc in range(4):
+            nc.tensor.transpose(turned[:, mc, :], wgs_raw[:, P * mc : P * mc + P], ident[:])
+        wide = tile([P, 4, 4, P], F32, "wide", tag="w1_raw01")
+        for c in range(4):
+            nc.scalar.copy(out=wide[:, :, :, 32 * c : 32 * c + 32].rearrange("m x t (q i) -> m x t q i", i=8),
+                           in_=turned[:].rearrange("m x (q t i) -> m x t q i", t=4, i=8))
+        for t in range(4):
+            back = ps.tile([P, 4, P], F32, name="back", tag="e", bufs=4)
+            for mc in range(4):
+                nc.tensor.transpose(back[:, mc, :], wide[:, mc, t, :], ident[:])
+            nc.scalar.copy(out=wgs_t[:, t, :], in_=back[:].rearrange("p x m -> p (x m)"))
+
+        gain_ps = ps.tile([P, P], F32, name="gain_ps", tag="e", bufs=4)
+        nc.tensor.transpose(gain_ps[:], gain_rows[:], ident[:])
+        nc.scalar.copy(out=gain_t[:], in_=gain_ps[:, 0:8])
 
         w1_raw = {}
         brief_t = {}
@@ -97,24 +124,22 @@ def tile_list_accord_slot_max_kernel(tc, tab_words, tab_scales, tab2_words, tab2
             brief_t[t] = rows[:]
 
         load_brief_lo(0)
-        load_brief_lo(1)
 
-        w2_c = tile([P, H], I32, "w2_c")
+        w2_c = tile([P, H], U32, "w2_c")
         w3_c = tile([P, H], U16, "w3_c")
         w23_cs = tile([P, H], U8, "w23_cs")
 
         def deal(dst, src, run):
-            nc.vector.tensor_copy(out=dst[:].rearrange("p (b t m i) -> p b m t i", b=2, t=4, i=run),
-                                  in_=src[:].rearrange("p (b m i t) -> p b m t i", b=2, t=4, i=run))
-
-        deal(w2_c, w2_raw, 4)
-        deal(w3_c, w3_raw, 8)
-        deal(w23_cs, w23_s, 16)
+            nc.vector.tensor_copy(out=dst[:].bitcast(I32).rearrange("p (b t q i) -> p b t q i", b=2, t=4, i=run),
+                                  in_=src[:].bitcast(I32).rearrange("p (b q t i) -> p b t q i", b=2, t=4, i=run))
 
         v2_w = tile([P, M], U32, "v2_w")
         v2_s = tile([P, M], U8, "v2_s")
         nc.vector.tensor_copy(v2_w[:], tab2_w[:].bitcast(U32).indirect(idx2[:]))
         nc.vector.tensor_copy(v2_s[:], tab2_s[:].indirect(idx2[:]))
+        deal(w23_cs, w23_s, 2)
+        deal(w3_c, w3_raw, 4)
+        deal(w2_c, w2_raw, 8)
 
         b_t = {}
 
@@ -128,12 +153,12 @@ def tile_list_accord_slot_max_kernel(tc, tab_words, tab_scales, tab2_words, tab2
                                 rhs=v2_w[:].bitcast(FP8X4), rhs_scale=v2_s[:], start=True, stop=True)
             th = tile([P, M], F32, "th", bufs=2)
             nc.scalar.activation(out=th[:], in_=arg[:], func=ACT.Tanh, scale=-1.0)
-            b = tile([P, M], F32, "b%d" % s, tag="w1_bf01" if s == 1 else None)
-            nc.vector.scalar_tensor_tensor(out=b[:], in0=th[:], scalar=gain_t[:, s // 4, s % 4 : s % 4 + 1], in1=lin[:],
+            b = tile([P, M], F32, "b%d" % s, tag="w1_bf01" if s == 4 else None)
+            nc.vector.scalar_tensor_tensor(out=b[:], in0=th[:], scalar=gain_t[:, s : s + 1], in1=lin[:],
                                            op0=ALU.mult, op1=ALU.add)
             b_t[s] = b
 
-        for s in (0, 2, 3, 4, 5, 6, 7):
+        for s in (0, 1, 2, 3, 5, 6, 7):
             accord(s)
 
         v_w = [tile([P, S], U32, "v_w%d" % a) for a in range(2)]
@@ -146,10 +171,12 @@ def tile_list_accord_slot_max_kernel(tc, tab_words, tab_scales, tab2_words, tab2
         for a in range(2):
             load_w1(1, a, w1_hi[:, a])
             w1_raw[1, a] = w1_hi[:, a]
-        load_brief_lo(2)
-        load_brief_lo(3)
         w4_raw = tile([P, 2, 4, N], F32, "w4_raw", tag="tab2_w4")
-        nc.sync.dma_start(out=w4_raw[:], in_=w4.rearrange("(b p j) n -> p b j n", b=2, j=4))
+        for b in range(2):
+            for t in range(4):
+                nc.sync.dma_start(out=w4_raw[:, b, t, :], in_=w4[512 * b : 512 * b + 512, :].rearrange("(q t i) n -> t q i n", t=4, i=8)[t])
+        for t in range(1, 4):
+            load_brief_lo(t)
         brief_hi = tile([P, 4, S], F32, "brief_hi", tag="big1")
         for t in range(4):
             load_brief(1, t, brief_hi[:, t, :])
@@ -161,24 +188,24 @@ def tile_list_accord_slot_max_kernel(tc, tab_words, tab_scales, tab2_words, tab2
         def quantise_w1(b):
             for a in range(2):
                 rounded = tile([P, 2048], BF16, "w1_bf%d%d" % (b, a), tag="w1_bf%d%d" % (b, a))
-                dst = rounded[:].rearrange("p (t m j) -> p m t j", t=4, j=4)
-                src = w1_raw[b, a].rearrange("p j (m t) -> p m t j", t=4)
-                for h in range(2):
-                    nc.scalar.copy(out=dst[:, 64 * h : 64 * h + 64], in_=src[:, 64 * h : 64 * h + 64])
+                dst = rounded[:].rearrange("p (t q h i j) -> p t q h j i", t=4, h=2, i=4, j=4)
+                src = w1_raw[b, a].rearrange("p j (q t h i) -> p t q h j i", t=4, h=2, i=4)
+                for t in range(4):
+                    nc.scalar.copy(out=dst[:, t], in_=src[:, t])
                 w1_c[b, a] = tile([P, 512], U32, "w1_c%d%d" % (b, a))
                 w1_s[b, a] = tile([P, 512], U8, "w1_s%d%d" % (b, a))
                 nc.vector.quantize_mx(out=w1_c[b, a][:].bitcast(FP8X4), scales=w1_s[b, a][:], in_=rounded[:])
 
         quantise_w1(0)
 
-        accord(1)
+        accord(4)
 
         def place(s):
-            nc.vector.tensor_tensor(pages[s % 2][:].indirect(slot[:]), b_t[s][:], wgs_t[:, s % 4, :], ALU.mult)
+            nc.vector.tensor_tensor(pages[s % 5][:].indirect(slot[:]), b_t[s][:], wgs_t[:, s % 4, :], ALU.mult)
 
         def gate(s):
             b, t = divmod(s, 4)
-            sig = tile([P, S], F32, "sig", bufs=3)
+            sig = tile([P, S], F32, "sig", bufs=4)
             cols = slice(P * t, P * t + P)
             for h in range(2):
                 e = ps.tile([P, BANK], F32, name="e", tag="e", bufs=4)
@@ -189,29 +216,19 @@ def tile_list_accord_slot_max_kernel(tc, tab_words, tab_scales, tab2_words, tab2
                 nc.scalar.activation(out=sig[:, js], in_=e[:], func=ACT.Sigmoid)
             nc.vector.tensor_tensor(out=brief_t[s], in0=brief_t[s], in1=sig[:], op=ALU.mult)
 
-        z_lo = tile([P, 4, S], BF16, "z_lo")
+        z_lo = tile([P, 4, S], BF16, "z_lo", tag="w1_raw00")
         z_hi = [tile([P, 4, CHUNK], BF16, "z_hi%d" % c) for c in range(4)]
 
-        def larger(s):
-            b, t = divmod(s, 4)
-            if b == 0:
-                nc.vector.tensor_tensor(out=z_lo[:, t, :], in0=brief_t[s], in1=pages[s % 2][:], op=ALU.max)
-            else:
-                for c in range(4):
-                    js = slice(CHUNK * c, CHUNK * c + CHUNK)
-                    nc.vector.tensor_tensor(out=z_hi[c][:, t, :], in0=brief_t[s][:, js], in1=pages[s % 2][:, js], op=ALU.max)
-
-        for s in range(2):
+        for s in range(5):
+            nc.vector.memset(pages[s][:], 0.0)
             place(s)
-        for s in range(2):
+        for s in range(4):
             gate(s)
-        for s in range(8):
-            larger(s)
-            if s + 2 == 4:
-                quantise_w1(1)
-            if s + 2 < 8:
-                gate(s + 2)
-                place(s + 2)
+        for s in range(4):
+            nc.vector.tensor_tensor(out=z_lo[:, s, :], in0=brief_t[s], in1=pages[s][:], op=ALU.max)
+            if s + 5 < 8:
+                place(s + 5)
+        quantise_w1(1)
 
         z_c = {}
         z_s = {}
@@ -223,9 +240,6 @@ def tile_list_accord_slot_max_kernel(tc, tab_words, tab_scales, tab2_words, tab2
             z_s[b, c] = tile([P, CHUNK], U8, "z_s%d%d" % (b, c))
             nc.vector.quantize_mx(out=z_c[b, c][:].bitcast(FP8X4), scales=z_s[b, c][:], in_=woven[:])
 
-        for c in range(4):
-            quantise_z(0, c, z_lo[:, :, CHUNK * c : CHUNK * c + CHUNK], nc.scalar.copy)
-
         w4_bf = tile([P, 2, 4 * N], BF16, "w4_bf")
         for b in range(2):
             nc.scalar.copy(out=w4_bf[:, b, :].rearrange("p (c i j) -> p c j i", i=4, j=4), in_=w4_raw[:, b].rearrange("p j (c i) -> p c j i", i=4))
@@ -233,18 +247,27 @@ def tile_list_accord_slot_max_kernel(tc, tab_words, tab_scales, tab2_words, tab2
         w4_s = tile([P, 2 * N], U8, "w4_s")
         nc.vector.quantize_mx(out=w4_c[:].bitcast(FP8X4), scales=w4_s[:], in_=w4_bf[:].rearrange("p b x -> p (b x)"))
 
+        for s in range(4, 8):
+            gate(s)
         for c in range(4):
-            quantise_z(1, c, z_hi[c][:], nc.scalar.copy if c < 2 else nc.vector.tensor_copy)
+            quantise_z(0, c, z_lo[:, :, CHUNK * c : CHUNK * c + CHUNK], nc.scalar.copy)
+
         for c in range(4):
-            acc = ps.tile([P, 2, CHUNK], F32, name="acc", tag="lin" if c % 2 == 0 else "arg")
-            for n in range(2):
-                for b in range(2):
+            js = slice(CHUNK * c, CHUNK * c + CHUNK)
+            for t in range(4):
+                nc.vector.tensor_tensor(out=z_hi[c][:, t, :], in0=brief_t[4 + t][:, js], in1=pages[(4 + t) % 5][:, js], op=ALU.max)
+            quantise_z(1, c, z_hi[c][:], nc.scalar.copy if c < 3 else nc.vector.tensor_copy)
+        for c in range(4):
+            acc = [ps.tile([P, CHUNK], F32, name="acc%d" % n, tag=("lin", "arg")[n]) for n in range(2)]
+            for b in range(2):
+                for n in range(2):
                     cols = slice(N * b + P * n, N * b + P * n + P)
-                    nc.tensor.matmul_mx(out=acc[:, n, :], lhsT=w4_c[:, cols].bitcast(FP8X4), lhsT_scale=w4_s[:, cols],
+                    nc.tensor.matmul_mx(out=acc[n][:], lhsT=w4_c[:, cols].bitcast(FP8X4), lhsT_scale=w4_s[:, cols],
                                         rhs=z_c[b, c][:].bitcast(FP8X4), rhs_scale=z_s[b, c][:], start=(b == 0), stop=(b == 1))
             res = tile([P, 2, CHUNK], F32, "res", bufs=4)
-            if c % 2 == 0:
-                nc.scalar.copy(out=res[:], in_=acc[:])
+            nc.scalar.copy(out=res[:, 0, :], in_=acc[0][:])
+            if c < 3:
+                nc.scalar.copy(out=res[:, 1, :], in_=acc[1][:])
             else:
-                nc.vector.tensor_copy(out=res[:], in_=acc[:])
+                nc.vector.tensor_copy(out=res[:, 1, :], in_=acc[1][:])
             nc.sync.dma_start(out=out[:, CHUNK * c : CHUNK * c + CHUNK].rearrange("(n p) j -> p n j", n=2), in_=res[:])

@@ -16,9 +16,19 @@ ACT = mybir.ActivationFunctionType
 
 T, S, T2, M, K, K2, H, N = 4096, 1024, 2048, 512, 1024, 512, 1024, 256
 FLOPS = 2 * K * H * S + 2 * 2 * K2 * H * M + 2 * H * N * S
+
 P = 128
+PASS = 512
+PACK = 4
+RUN = 8
 BANK = 512
+SLICES = H // P
 CHUNK = 256
+CHUNKS = S // CHUNK
+PAGES = 5
+HELD = PAGES - 1
+BRIEF_FIRST = 2
+RING = 6
 
 
 def tile_list_accord_slot_max_kernel(tc, tab_words, tab_scales, tab2_words, tab2_scales, offs, offs2, pos1, w1,
@@ -32,134 +42,139 @@ def tile_list_accord_slot_max_kernel(tc, tab_words, tab_scales, tab2_words, tab2
         def tile(shape, dtype, name, tag=None, bufs=1):
             return sb.tile(shape, dtype, name=name, tag=tag or name, bufs=bufs, align_bytes=64)
 
+        def ring_bank(shape, name):
+            return ps.tile(shape, F32, name=name, tag="ring", bufs=RING)
+
         idx = lists.tile([P, S // 16], U16, name="idx")
         idx2 = lists.tile([P, M // 16], U16, name="idx2")
-        slot = lists.tile([P, M // 16], U16, name="slot")
+        p1 = lists.tile([P, M // 16], U16, name="p1")
 
         tab2_s = tile([P, T2], U8, "tab2_s")
         w23_s = tile([P, H], U8, "w23_s")
         tab_s = tile([P, T], U8, "tab_s")
-        pages = [tile([P, S], F32, "page%d" % i) for i in range(5)]
+        pages = [tile([P, S], F32, "page%d" % n) for n in range(PAGES)]
         nc.vector.memset(tab2_s[:].bitcast(I32), 0)
         nc.vector.memset(w23_s[:].bitcast(I32), 0)
         nc.vector.memset(tab_s[:].bitcast(I32), 0)
 
         w2_raw = tile([P, H], U32, "w2_raw")
         w3_raw = tile([P, H], U16, "w3_raw")
-        tab2_w = tile([P, T2], I32, "tab2_w", tag="tab2_w4")
+        tab2_w = tile([P, T2], I32, "tab2_w", tag="tab2_then_w4")
         tab_w = [tile([P, T], I32, "tab_w%d" % a, tag="big%d" % a) for a in range(2)]
-        gain_t = tile([P, 8], F32, "gain_t")
+        gain_t = tile([P, SLICES], F32, "gain_t")
         gain_rows = tile([P, P], F32, "gain_rows")
         nc.gpsimd.memset(gain_rows[:], 0.0)
-        wgs_t = tile([P, 4, M], F32, "wgs_t")
+        wgs_t = tile([P, PACK, M], F32, "wgs_t")
         wgs_raw = tile([P, M], F32, "wgs_raw")
         ident = tile([P, P], F32, "ident")
         make_identity(nc, ident[:])
 
         def words(src):
-            return src.rearrange("p c i -> p (c i)").bitcast(I32)
+            return src.rearrange("p c j -> p (c j)").bitcast(I32)
 
-        def load_scale_rows(plane, first, src, r):
-            nc.sync.dma_start(out=plane[first + r : P : 32, :].bitcast(I32), in_=src[r : 16 : 4, :].bitcast(I32))
+        def load_scale_rows(scale_tile, first, src, u):
+            nc.sync.dma_start(out=scale_tile[first + u : P : 32, :].bitcast(I32), in_=src[u : 16 : 4, :].bitcast(I32))
 
-        for r in range(4):
-            load_scale_rows(tab2_s, 0, tab2_scales[0], r)
+        def pass_rows(src, b):
+            return src[PASS * b : PASS * b + PASS]
+
+        for u in range(4):
+            load_scale_rows(tab2_s, 0, tab2_scales[0], u)
         nc.sync.dma_start(out=wgs_raw[:], in_=wgs)
         nc.sync.dma_start(idx2[:], offs2)
         nc.sync.dma_start(out=tab2_w[:], in_=words(tab2_words[0]))
         nc.sync.dma_start(out=w2_raw[:].bitcast(I32), in_=words(w2_words[0]))
         nc.sync.dma_start(out=w3_raw[:].bitcast(I32), in_=w3_words[0].bitcast(I32))
-        for r in range(4):
-            load_scale_rows(w23_s, 0, w3_scales[0], r)
-            load_scale_rows(w23_s, 4, w2_scales[0], r)
+        for u in range(4):
+            load_scale_rows(w23_s, 0, w3_scales[0], u)
+            load_scale_rows(w23_s, 4, w2_scales[0], u)
         for b in range(2):
-            nc.sync.dma_start(out=gain_rows[4 * b : 4 * b + 4, :].rearrange("t (q i) -> t q i", i=8),
-                              in_=gain[512 * b : 512 * b + 512].rearrange("(q t i) -> t q i", t=4, i=8))
-        nc.sync.dma_start(slot[:], pos1)
+            nc.sync.dma_start(out=gain_rows[PACK * b : PACK * b + PACK, :].rearrange("t (q i) -> t q i", i=RUN),
+                              in_=pass_rows(gain, b).rearrange("(q t i) -> t q i", t=PACK, i=RUN))
+        nc.sync.dma_start(p1[:], pos1)
         nc.sync.dma_start(idx[:], offs)
-        nc.sync.dma_start(out=tab_w[0][:, : T // 2], in_=words(tab_words[0])[:, : T // 2])
-        nc.sync.dma_start(out=tab_w[0][:, T // 2 :], in_=words(tab_words[0])[:, T // 2 :])
-        for r in range(2):
-            for a in range(2):
-                load_scale_rows(tab_s, 4 * a, tab_scales[a], r)
-        nc.sync.dma_start(out=tab_w[1][:, : T // 2], in_=words(tab_words[1])[:, : T // 2])
-        for r in range(2, 4):
-            for a in range(2):
-                load_scale_rows(tab_s, 4 * a, tab_scales[a], r)
-        nc.sync.dma_start(out=tab_w[1][:, T // 2 :], in_=words(tab_words[1])[:, T // 2 :])
+        halves = (slice(0, T // 2), slice(T // 2, T))
+        for cols in halves:
+            nc.sync.dma_start(out=tab_w[0][:, cols], in_=words(tab_words[0])[:, cols])
+        for h, cols in enumerate(halves):
+            for u in (2 * h, 2 * h + 1):
+                for a in range(2):
+                    load_scale_rows(tab_s, 4 * a, tab_scales[a], u)
+            nc.sync.dma_start(out=tab_w[1][:, cols], in_=words(tab_words[1])[:, cols])
 
         def load_w1(b, a, dst):
-            nc.sync.dma_start(out=dst, in_=w1[512 * a : 512 * a + 512, 512 * b : 512 * b + 512].rearrange("(p j) c -> p j c", j=4))
+            nc.sync.dma_start(out=dst, in_=pass_rows(w1, a)[:, PASS * b : PASS * b + PASS].rearrange("(p j) c -> p j c", j=PACK))
 
-        def load_brief(b, t, dst):
-            nc.sync.dma_start(out=dst, in_=brief[512 * b : 512 * b + 512, :].rearrange("(q t i) j -> t q i j", t=4, i=8)[t])
+        def load_slice(src, b, t, dst):
+            nc.sync.dma_start(out=dst, in_=pass_rows(src, b).rearrange("(q t i) c -> t q i c", t=PACK, i=RUN)[t])
 
-        turned = ps.tile([P, 4, P], F32, name="turned", tag="e", bufs=4)
-        for mc in range(4):
-            nc.tensor.transpose(turned[:, mc, :], wgs_raw[:, P * mc : P * mc + P], ident[:])
-        wide = tile([P, 4, 4, P], F32, "wide", tag="w1_raw01")
+        wgs_turned = ring_bank([P, 4, P], "wgs_turned")
+        for x in range(4):
+            nc.tensor.transpose(wgs_turned[:, x, :], wgs_raw[:, P * x : P * x + P], ident[:])
+        wgs_dealt = tile([P, 4, PACK, P], F32, "wgs_dealt", tag="w1_raw01")
         for c in range(4):
-            nc.scalar.copy(out=wide[:, :, :, 32 * c : 32 * c + 32].rearrange("m x t (q i) -> m x t q i", i=8),
-                           in_=turned[:].rearrange("m x (q t i) -> m x t q i", t=4, i=8))
-        for t in range(4):
-            back = ps.tile([P, 4, P], F32, name="back", tag="e", bufs=4)
-            for mc in range(4):
-                nc.tensor.transpose(back[:, mc, :], wide[:, mc, t, :], ident[:])
-            nc.scalar.copy(out=wgs_t[:, t, :], in_=back[:].rearrange("p x m -> p (x m)"))
+            nc.scalar.copy(out=wgs_dealt[:, :, :, 32 * c : 32 * c + 32].rearrange("m x t (q i) -> m x t q i", i=RUN),
+                           in_=wgs_turned[:].rearrange("m x (q t i) -> m x t q i", t=PACK, i=RUN))
+        for t in range(PACK):
+            wgs_back = ring_bank([P, 4, P], "wgs_back")
+            for x in range(4):
+                nc.tensor.transpose(wgs_back[:, x, :], wgs_dealt[:, x, t, :], ident[:])
+            nc.scalar.copy(out=wgs_t[:, t, :], in_=wgs_back[:].rearrange("p x m -> p (x m)"))
 
-        gain_ps = ps.tile([P, P], F32, name="gain_ps", tag="e", bufs=4)
-        nc.tensor.transpose(gain_ps[:], gain_rows[:], ident[:])
-        nc.scalar.copy(out=gain_t[:], in_=gain_ps[:, 0:8])
+        gain_turned = ring_bank([P, P], "gain_turned")
+        nc.tensor.transpose(gain_turned[:], gain_rows[:], ident[:])
+        nc.scalar.copy(out=gain_t[:], in_=gain_turned[:, 0:SLICES])
 
         w1_raw = {}
-        brief_t = {}
+        a_t = {}
         for a in range(2):
-            raw = tile([P, 4, 512], F32, "w1_raw0%d" % a)
+            raw = tile([P, PACK, PASS], F32, "w1_raw0%d" % a)
             load_w1(0, a, raw[:])
             w1_raw[0, a] = raw[:]
 
         def load_brief_lo(t):
             rows = tile([P, S], F32, "brief0%d" % t)
-            load_brief(0, t, rows[:])
-            brief_t[t] = rows[:]
+            load_slice(brief, 0, t, rows[:])
+            a_t[t] = rows[:]
 
-        load_brief_lo(0)
+        for t in range(BRIEF_FIRST):
+            load_brief_lo(t)
 
         w2_c = tile([P, H], U32, "w2_c")
         w3_c = tile([P, H], U16, "w3_c")
         w23_cs = tile([P, H], U8, "w23_cs")
 
-        def deal(dst, src, run):
-            nc.vector.tensor_copy(out=dst[:].bitcast(I32).rearrange("p (b t q i) -> p b t q i", b=2, t=4, i=run),
-                                  in_=src[:].bitcast(I32).rearrange("p (b q t i) -> p b t q i", b=2, t=4, i=run))
+        def deal(dst, src, run_words):
+            nc.vector.tensor_copy(out=dst[:].bitcast(I32).rearrange("p (b t q w) -> p b t q w", b=2, t=PACK, w=run_words),
+                                  in_=src[:].bitcast(I32).rearrange("p (b q t w) -> p b t q w", b=2, t=PACK, w=run_words))
 
         v2_w = tile([P, M], U32, "v2_w")
         v2_s = tile([P, M], U8, "v2_s")
         nc.vector.tensor_copy(v2_w[:], tab2_w[:].bitcast(U32).indirect(idx2[:]))
         nc.vector.tensor_copy(v2_s[:], tab2_s[:].indirect(idx2[:]))
-        deal(w23_cs, w23_s, 2)
-        deal(w3_c, w3_raw, 4)
-        deal(w2_c, w2_raw, 8)
+        deal(w23_cs, w23_s, RUN // 4)
+        deal(w3_c, w3_raw, RUN // 2)
+        deal(w2_c, w2_raw, RUN)
 
         b_t = {}
 
         def accord(s):
             cols = slice(P * s, P * s + P)
-            lin = ps.tile([P, M], F32, name="lin", tag="lin")
+            lin = ring_bank([P, M], "lin")
             arg = ps.tile([P, M], F32, name="arg", tag="arg")
             nc.tensor.matmul_mx(out=arg[:], lhsT=w3_c[:, cols].bitcast(FP4X4), lhsT_scale=w23_cs[:, cols],
                                 rhs=v2_w[:].bitcast(FP8X4), rhs_scale=v2_s[:], start=True, stop=True)
             nc.tensor.matmul_mx(out=lin[:], lhsT=w2_c[:, cols].bitcast(FP8X4), lhsT_scale=w23_cs[4:P, cols],
                                 rhs=v2_w[:].bitcast(FP8X4), rhs_scale=v2_s[:], start=True, stop=True)
-            th = tile([P, M], F32, "th", bufs=2)
+            b_s = tile([P, M], F32, "b%d" % s, tag="w1_bf01" if s == HELD else None)
+            th = tile([P, M], F32, "th_held") if s == HELD else b_s
             nc.scalar.activation(out=th[:], in_=arg[:], func=ACT.Tanh, scale=-1.0)
-            b = tile([P, M], F32, "b%d" % s, tag="w1_bf01" if s == 4 else None)
-            nc.vector.scalar_tensor_tensor(out=b[:], in0=th[:], scalar=gain_t[:, s : s + 1], in1=lin[:],
-                                           op0=ALU.mult, op1=ALU.add)
-            b_t[s] = b
+            nc.vector.scalar_tensor_tensor(out=b_s[:], in0=th[:], scalar=gain_t[:, s : s + 1], in1=lin[:], op0=ALU.mult, op1=ALU.add)
+            b_t[s] = b_s
 
-        for s in (0, 1, 2, 3, 5, 6, 7):
-            accord(s)
+        for s in range(SLICES):
+            if s != HELD:
+                accord(s)
 
         v_w = [tile([P, S], U32, "v_w%d" % a) for a in range(2)]
         v_s = tile([P, S], U8, "v_s")
@@ -167,107 +182,109 @@ def tile_list_accord_slot_max_kernel(tc, tab_words, tab_scales, tab2_words, tab2
         nc.vector.tensor_copy(v_s[:], tab_s[:].indirect(idx[:]))
         nc.vector.tensor_copy(v_w[1][:], tab_w[1][:].bitcast(U32).indirect(idx[:]))
 
-        w1_hi = tile([P, 2, 4, 512], F32, "w1_hi", tag="big0")
+        w1_hi = tile([P, 2, PACK, PASS], F32, "w1_hi", tag="big0")
         for a in range(2):
             load_w1(1, a, w1_hi[:, a])
             w1_raw[1, a] = w1_hi[:, a]
-        w4_raw = tile([P, 2, 4, N], F32, "w4_raw", tag="tab2_w4")
+        w4_raw = tile([P, 2, PACK, N], F32, "w4_raw", tag="tab2_then_w4")
         for b in range(2):
-            for t in range(4):
-                nc.sync.dma_start(out=w4_raw[:, b, t, :], in_=w4[512 * b : 512 * b + 512, :].rearrange("(q t i) n -> t q i n", t=4, i=8)[t])
-        for t in range(1, 4):
+            for t in range(PACK):
+                load_slice(w4, b, t, w4_raw[:, b, t, :])
+        for t in range(BRIEF_FIRST, PACK):
             load_brief_lo(t)
-        brief_hi = tile([P, 4, S], F32, "brief_hi", tag="big1")
-        for t in range(4):
-            load_brief(1, t, brief_hi[:, t, :])
-            brief_t[4 + t] = brief_hi[:, t, :]
+        brief_hi = tile([P, PACK, S], F32, "brief_hi", tag="big1")
+        for t in range(PACK):
+            load_slice(brief, 1, t, brief_hi[:, t, :])
+            a_t[PACK + t] = brief_hi[:, t, :]
 
         w1_c = {}
         w1_s = {}
 
         def quantise_w1(b):
             for a in range(2):
-                rounded = tile([P, 2048], BF16, "w1_bf%d%d" % (b, a), tag="w1_bf%d%d" % (b, a))
-                dst = rounded[:].rearrange("p (t q h i j) -> p t q h j i", t=4, h=2, i=4, j=4)
-                src = w1_raw[b, a].rearrange("p j (q t h i) -> p t q h j i", t=4, h=2, i=4)
-                for t in range(4):
+                rounded = tile([P, PACK * PASS], BF16, "w1_bf%d%d" % (b, a))
+                dst = rounded[:].rearrange("p (t q h l j) -> p t q h j l", t=PACK, h=2, l=4, j=PACK)
+                src = w1_raw[b, a].rearrange("p j (q t h l) -> p t q h j l", t=PACK, h=2, l=4)
+                for t in range(PACK):
                     nc.scalar.copy(out=dst[:, t], in_=src[:, t])
-                w1_c[b, a] = tile([P, 512], U32, "w1_c%d%d" % (b, a))
-                w1_s[b, a] = tile([P, 512], U8, "w1_s%d%d" % (b, a))
+                w1_c[b, a] = tile([P, PASS], U32, "w1_c%d%d" % (b, a))
+                w1_s[b, a] = tile([P, PASS], U8, "w1_s%d%d" % (b, a))
                 nc.vector.quantize_mx(out=w1_c[b, a][:].bitcast(FP8X4), scales=w1_s[b, a][:], in_=rounded[:])
 
         quantise_w1(0)
-
-        accord(4)
+        accord(HELD)
 
         def place(s):
-            nc.vector.tensor_tensor(pages[s % 5][:].indirect(slot[:]), b_t[s][:], wgs_t[:, s % 4, :], ALU.mult)
+            nc.vector.tensor_tensor(pages[s % PAGES][:].indirect(p1[:]), b_t[s][:], wgs_t[:, s % PACK, :], ALU.mult)
 
         def gate(s):
-            b, t = divmod(s, 4)
-            sig = tile([P, S], F32, "sig", bufs=4)
+            b, t = divmod(s, PACK)
+            sig = tile([P, S], F32, "sig", bufs=PACK)
             cols = slice(P * t, P * t + P)
-            for h in range(2):
-                e = ps.tile([P, BANK], F32, name="e", tag="e", bufs=4)
+            for h in range(S // BANK):
+                e = ring_bank([P, BANK], "e")
                 js = slice(BANK * h, BANK * h + BANK)
                 for a in range(2):
                     nc.tensor.matmul_mx(out=e[:], lhsT=w1_c[b, a][:, cols].bitcast(FP8X4), lhsT_scale=w1_s[b, a][:, cols],
                                         rhs=v_w[a][:, js].bitcast(FP8X4), rhs_scale=v_s[4 * a : P, js], start=(a == 0), stop=(a == 1))
                 nc.scalar.activation(out=sig[:, js], in_=e[:], func=ACT.Sigmoid)
-            nc.vector.tensor_tensor(out=brief_t[s], in0=brief_t[s], in1=sig[:], op=ALU.mult)
+            nc.vector.tensor_tensor(out=a_t[s], in0=a_t[s], in1=sig[:], op=ALU.mult)
 
-        z_lo = tile([P, 4, S], BF16, "z_lo", tag="w1_raw00")
-        z_hi = [tile([P, 4, CHUNK], BF16, "z_hi%d" % c) for c in range(4)]
+        z_lo = tile([P, PACK, S], BF16, "z_lo", tag="w1_raw00")
+        z_hi = [tile([P, PACK, CHUNK], BF16, "z_hi%d" % c) for c in range(CHUNKS)]
 
-        for s in range(5):
+        for s in range(PAGES):
             nc.vector.memset(pages[s][:], 0.0)
             place(s)
-        for s in range(4):
+        for s in range(PACK):
             gate(s)
-        for s in range(4):
-            nc.vector.tensor_tensor(out=z_lo[:, s, :], in0=brief_t[s], in1=pages[s][:], op=ALU.max)
-            if s + 5 < 8:
-                place(s + 5)
+        for s in range(PACK):
+            nc.vector.tensor_tensor(out=z_lo[:, s, :], in0=a_t[s], in1=pages[s][:], op=ALU.max)
+            if s > 0:
+                place(s - 1 + PAGES)
         quantise_w1(1)
 
         z_c = {}
         z_s = {}
 
         def quantise_z(b, c, src, copy):
-            woven = tile([P, 4 * CHUNK], BF16, "woven", bufs=4)
-            copy(out=woven[:].rearrange("p (c i t) -> p c t i", i=4, t=4), in_=src.rearrange("p t (c i) -> p c t i", i=4))
+            woven = tile([P, PACK * CHUNK], BF16, "woven", bufs=CHUNKS)
+            copy(out=woven[:].rearrange("p (g l t) -> p g t l", l=4, t=PACK), in_=src.rearrange("p t (g l) -> p g t l", l=4))
             z_c[b, c] = tile([P, CHUNK], U32, "z_c%d%d" % (b, c))
             z_s[b, c] = tile([P, CHUNK], U8, "z_s%d%d" % (b, c))
             nc.vector.quantize_mx(out=z_c[b, c][:].bitcast(FP8X4), scales=z_s[b, c][:], in_=woven[:])
 
-        w4_bf = tile([P, 2, 4 * N], BF16, "w4_bf")
+        w4_bf = tile([P, 2, PACK * N], BF16, "w4_bf")
         for b in range(2):
-            nc.scalar.copy(out=w4_bf[:, b, :].rearrange("p (c i j) -> p c j i", i=4, j=4), in_=w4_raw[:, b].rearrange("p j (c i) -> p c j i", i=4))
+            nc.scalar.copy(out=w4_bf[:, b, :].rearrange("p (g l t) -> p g t l", l=4, t=PACK),
+                           in_=w4_raw[:, b].rearrange("p t (g l) -> p g t l", l=4))
         w4_c = tile([P, 2 * N], U32, "w4_c")
         w4_s = tile([P, 2 * N], U8, "w4_s")
         nc.vector.quantize_mx(out=w4_c[:].bitcast(FP8X4), scales=w4_s[:], in_=w4_bf[:].rearrange("p b x -> p (b x)"))
 
-        for s in range(4, 8):
+        for s in range(PACK, SLICES):
             gate(s)
-        for c in range(4):
+        for c in range(CHUNKS):
             quantise_z(0, c, z_lo[:, :, CHUNK * c : CHUNK * c + CHUNK], nc.scalar.copy)
 
-        for c in range(4):
+        last = CHUNKS - 1
+        for c in range(CHUNKS):
             js = slice(CHUNK * c, CHUNK * c + CHUNK)
-            for t in range(4):
-                nc.vector.tensor_tensor(out=z_hi[c][:, t, :], in0=brief_t[4 + t][:, js], in1=pages[(4 + t) % 5][:, js], op=ALU.max)
-            quantise_z(1, c, z_hi[c][:], nc.scalar.copy if c < 3 else nc.vector.tensor_copy)
-        for c in range(4):
-            acc = [ps.tile([P, CHUNK], F32, name="acc%d" % n, tag=("lin", "arg")[n]) for n in range(2)]
+            for t in range(PACK):
+                s = PACK + t
+                nc.vector.tensor_tensor(out=z_hi[c][:, t, :], in0=a_t[s][:, js], in1=pages[s % PAGES][:, js], op=ALU.max)
+            quantise_z(1, c, z_hi[c][:], nc.vector.tensor_copy if c == last else nc.scalar.copy)
+        for c in range(CHUNKS):
+            acc = [ps.tile([P, CHUNK], F32, name="acc0", tag="arg"), ring_bank([P, CHUNK], "acc1")]
             for b in range(2):
                 for n in range(2):
                     cols = slice(N * b + P * n, N * b + P * n + P)
                     nc.tensor.matmul_mx(out=acc[n][:], lhsT=w4_c[:, cols].bitcast(FP8X4), lhsT_scale=w4_s[:, cols],
                                         rhs=z_c[b, c][:].bitcast(FP8X4), rhs_scale=z_s[b, c][:], start=(b == 0), stop=(b == 1))
-            res = tile([P, 2, CHUNK], F32, "res", bufs=4)
+            res = tile([P, 2, CHUNK], F32, "res", bufs=CHUNKS)
             nc.scalar.copy(out=res[:, 0, :], in_=acc[0][:])
-            if c < 3:
-                nc.scalar.copy(out=res[:, 1, :], in_=acc[1][:])
-            else:
+            if c == last:
                 nc.vector.tensor_copy(out=res[:, 1, :], in_=acc[1][:])
+            else:
+                nc.scalar.copy(out=res[:, 1, :], in_=acc[1][:])
             nc.sync.dma_start(out=out[:, CHUNK * c : CHUNK * c + CHUNK].rearrange("(n p) j -> p n j", n=2), in_=res[:])

from contextlib import ExitStack

import concourse.mybir as mybir
from concourse.masks import make_identity

F32 = mybir.dt.float32
BF16 = mybir.dt.bfloat16
I32 = mybir.dt.int32
U32 = mybir.dt.uint32
U16 = mybir.dt.uint16
U8 = mybir.dt.uint8
FP8X4 = mybir.dt.float8_e4m3fn_x4
FP4X4 = mybir.dt.float4_e2m1fn_x4
ALU = mybir.AluOpType
ACT = mybir.ActivationFunctionType

T, S, T2, M, K, K2, H, N = 4096, 1024, 2048, 512, 1024, 512, 1024, 256
FLOPS = 2 * K * H * S + 2 * 2 * K2 * H * M + 2 * H * N * S

P = 128
PASS = 512
PACK = 4
RUN = 8
BANK = 512
SLICES = H // P
CHUNK = 256
CHUNKS = S // CHUNK
PAGES = 5
HELD = PAGES - 1
BRIEF_FIRST = 2
RING = 6


def tile_list_accord_slot_max_kernel(tc, tab_words, tab_scales, tab2_words, tab2_scales, offs, offs2, pos1, w1,
                                              w2_words, w2_scales, w3_words, w3_scales, w4, brief, gain, wgs, out):
    nc = tc.nc
    with ExitStack() as ctx:
        lists = ctx.enter_context(tc.tile_pool(name="lists", bufs=1))
        sb = ctx.enter_context(tc.tile_pool(name="sb", bufs=1))
        ps = ctx.enter_context(tc.psum_pool(name="ps", bufs=2))

        def tile(shape, dtype, name, tag=None, bufs=1):
            return sb.tile(shape, dtype, name=name, tag=tag or name, bufs=bufs, align_bytes=64)

        def ring_bank(shape, name):
            return ps.tile(shape, F32, name=name, tag="ring", bufs=RING)

        idx = lists.tile([P, S // 16], U16, name="idx")
        idx2 = lists.tile([P, M // 16], U16, name="idx2")
        p1 = lists.tile([P, M // 16], U16, name="p1")

        tab2_s = tile([P, T2], U8, "tab2_s")
        w23_s = tile([P, H], U8, "w23_s")
        tab_s = tile([P, T], U8, "tab_s")
        pages = [tile([P, S], F32, "page%d" % n) for n in range(PAGES)]
        nc.vector.memset(tab2_s[:].bitcast(I32), 0)
        nc.vector.memset(w23_s[:].bitcast(I32), 0)
        nc.vector.memset(tab_s[:].bitcast(I32), 0)

        w2_raw = tile([P, H], U32, "w2_raw")
        w3_raw = tile([P, H], U16, "w3_raw")
        tab2_w = tile([P, T2], I32, "tab2_w", tag="tab2_then_w4")
        tab_w = [tile([P, T], I32, "tab_w%d" % a, tag="big%d" % a) for a in range(2)]
        gain_t = tile([P, SLICES], F32, "gain_t")
        gain_rows = tile([P, P], F32, "gain_rows")
        nc.gpsimd.memset(gain_rows[:], 0.0)
        wgs_t = tile([P, PACK, M], F32, "wgs_t")
        wgs_raw = tile([P, M], F32, "wgs_raw")
        ident = tile([P, P], F32, "ident")
        make_identity(nc, ident[:])

        def words(src):
            return src.rearrange("p c j -> p (c j)").bitcast(I32)

        def load_scale_rows(scale_tile, first, src, u):
            nc.sync.dma_start(out=scale_tile[first + u : P : 32, :].bitcast(I32), in_=src[u : 16 : 4, :].bitcast(I32))

        def pass_rows(src, b):
            return src[PASS * b : PASS * b + PASS]

        for u in range(4):
            load_scale_rows(tab2_s, 0, tab2_scales[0], u)
        nc.sync.dma_start(out=wgs_raw[:], in_=wgs)
        nc.sync.dma_start(idx2[:], offs2)
        nc.sync.dma_start(out=tab2_w[:], in_=words(tab2_words[0]))
        nc.sync.dma_start(out=w2_raw[:].bitcast(I32), in_=words(w2_words[0]))
        nc.sync.dma_start(out=w3_raw[:].bitcast(I32), in_=w3_words[0].bitcast(I32))
        for u in range(4):
            load_scale_rows(w23_s, 0, w3_scales[0], u)
            load_scale_rows(w23_s, 4, w2_scales[0], u)
        for b in range(2):
            nc.sync.dma_start(out=gain_rows[PACK * b : PACK * b + PACK, :].rearrange("t (q i) -> t q i", i=RUN),
                              in_=pass_rows(gain, b).rearrange("(q t i) -> t q i", t=PACK, i=RUN))
        nc.sync.dma_start(p1[:], pos1)
        nc.sync.dma_start(idx[:], offs)
        halves = (slice(0, T // 2), slice(T // 2, T))
        for cols in halves:
            nc.sync.dma_start(out=tab_w[0][:, cols], in_=words(tab_words[0])[:, cols])
        for h, cols in enumerate(halves):
            for u in (2 * h, 2 * h + 1):
                for a in range(2):
                    load_scale_rows(tab_s, 4 * a, tab_scales[a], u)
            nc.sync.dma_start(out=tab_w[1][:, cols], in_=words(tab_words[1])[:, cols])

        def load_w1(b, a, dst):
            nc.sync.dma_start(out=dst, in_=pass_rows(w1, a)[:, PASS * b : PASS * b + PASS].rearrange("(p j) c -> p j c", j=PACK))

        def load_slice(src, b, t, dst):
            nc.sync.dma_start(out=dst, in_=pass_rows(src, b).rearrange("(q t i) c -> t q i c", t=PACK, i=RUN)[t])

        wgs_turned = ring_bank([P, 4, P], "wgs_turned")
        for x in range(4):
            nc.tensor.transpose(wgs_turned[:, x, :], wgs_raw[:, P * x : P * x + P], ident[:])
        wgs_dealt = tile([P, 4, PACK, P], F32, "wgs_dealt", tag="w1_raw01")
        for c in range(4):
            nc.scalar.copy(out=wgs_dealt[:, :, :, 32 * c : 32 * c + 32].rearrange("m x t (q i) -> m x t q i", i=RUN),
                           in_=wgs_turned[:].rearrange("m x (q t i) -> m x t q i", t=PACK, i=RUN))
        for t in range(PACK):
            wgs_back = ring_bank([P, 4, P], "wgs_back")
            for x in range(4):
                nc.tensor.transpose(wgs_back[:, x, :], wgs_dealt[:, x, t, :], ident[:])
            nc.scalar.copy(out=wgs_t[:, t, :], in_=wgs_back[:].rearrange("p x m -> p (x m)"))

        gain_turned = ring_bank([P, P], "gain_turned")
        nc.tensor.transpose(gain_turned[:], gain_rows[:], ident[:])
        nc.scalar.copy(out=gain_t[:], in_=gain_turned[:, 0:SLICES])

        w1_raw = {}
        a_t = {}
        for a in range(2):
            raw = tile([P, PACK, PASS], F32, "w1_raw0%d" % a)
            load_w1(0, a, raw[:])
            w1_raw[0, a] = raw[:]

        def load_brief_lo(t):
            rows = tile([P, S], F32, "brief0%d" % t)
            load_slice(brief, 0, t, rows[:])
            a_t[t] = rows[:]

        for t in range(BRIEF_FIRST):
            load_brief_lo(t)

        w2_c = tile([P, H], U32, "w2_c")
        w3_c = tile([P, H], U16, "w3_c")
        w23_cs = tile([P, H], U8, "w23_cs")

        def deal(dst, src, run_words):
            nc.vector.tensor_copy(out=dst[:].bitcast(I32).rearrange("p (b t q w) -> p b t q w", b=2, t=PACK, w=run_words),
                                  in_=src[:].bitcast(I32).rearrange("p (b q t w) -> p b t q w", b=2, t=PACK, w=run_words))

        v2_w = tile([P, M], U32, "v2_w")
        v2_s = tile([P, M], U8, "v2_s")
        nc.vector.tensor_copy(v2_w[:], tab2_w[:].bitcast(U32).indirect(idx2[:]))
        nc.vector.tensor_copy(v2_s[:], tab2_s[:].indirect(idx2[:]))
        deal(w23_cs, w23_s, RUN // 4)
        deal(w3_c, w3_raw, RUN // 2)
        deal(w2_c, w2_raw, RUN)

        b_t = {}

        def accord(s):
            cols = slice(P * s, P * s + P)
            lin = ring_bank([P, M], "lin")
            arg = ps.tile([P, M], F32, name="arg", tag="arg")
            nc.tensor.matmul_mx(out=arg[:], lhsT=w3_c[:, cols].bitcast(FP4X4), lhsT_scale=w23_cs[:, cols],
                                rhs=v2_w[:].bitcast(FP8X4), rhs_scale=v2_s[:], start=True, stop=True)
            nc.tensor.matmul_mx(out=lin[:], lhsT=w2_c[:, cols].bitcast(FP8X4), lhsT_scale=w23_cs[4:P, cols],
                                rhs=v2_w[:].bitcast(FP8X4), rhs_scale=v2_s[:], start=True, stop=True)
            b_s = tile([P, M], F32, "b%d" % s, tag="w1_bf01" if s == HELD else None)
            th = tile([P, M], F32, "th_held") if s == HELD else b_s
            nc.scalar.activation(out=th[:], in_=arg[:], func=ACT.Tanh, scale=-1.0)
            nc.vector.scalar_tensor_tensor(out=b_s[:], in0=th[:], scalar=gain_t[:, s : s + 1], in1=lin[:], op0=ALU.mult, op1=ALU.add)
            b_t[s] = b_s

        for s in range(SLICES):
            if s != HELD:
                accord(s)

        v_w = [tile([P, S], U32, "v_w%d" % a) for a in range(2)]
        v_s = tile([P, S], U8, "v_s")
        nc.vector.tensor_copy(v_w[0][:], tab_w[0][:].bitcast(U32).indirect(idx[:]))
        nc.vector.tensor_copy(v_s[:], tab_s[:].indirect(idx[:]))
        nc.vector.tensor_copy(v_w[1][:], tab_w[1][:].bitcast(U32).indirect(idx[:]))

        w1_hi = tile([P, 2, PACK, PASS], F32, "w1_hi", tag="big0")
        for a in range(2):
            load_w1(1, a, w1_hi[:, a])
            w1_raw[1, a] = w1_hi[:, a]
        w4_raw = tile([P, 2, PACK, N], F32, "w4_raw", tag="tab2_then_w4")
        for b in range(2):
            for t in range(PACK):
                load_slice(w4, b, t, w4_raw[:, b, t, :])
        for t in range(BRIEF_FIRST, PACK):
            load_brief_lo(t)
        brief_hi = tile([P, PACK, S], F32, "brief_hi", tag="big1")
        for t in range(PACK):
            load_slice(brief, 1, t, brief_hi[:, t, :])
            a_t[PACK + t] = brief_hi[:, t, :]

        w1_c = {}
        w1_s = {}

        def quantise_w1(b):
            for a in range(2):
                rounded = tile([P, PACK * PASS], BF16, "w1_bf%d%d" % (b, a))
                dst = rounded[:].rearrange("p (t q h l j) -> p t q h j l", t=PACK, h=2, l=4, j=PACK)
                src = w1_raw[b, a].rearrange("p j (q t h l) -> p t q h j l", t=PACK, h=2, l=4)
                for t in range(PACK):
                    nc.scalar.copy(out=dst[:, t], in_=src[:, t])
                w1_c[b, a] = tile([P, PASS], U32, "w1_c%d%d" % (b, a))
                w1_s[b, a] = tile([P, PASS], U8, "w1_s%d%d" % (b, a))
                nc.vector.quantize_mx(out=w1_c[b, a][:].bitcast(FP8X4), scales=w1_s[b, a][:], in_=rounded[:])

        quantise_w1(0)
        accord(HELD)

        def place(s):
            nc.vector.tensor_tensor(pages[s % PAGES][:].indirect(p1[:]), b_t[s][:], wgs_t[:, s % PACK, :], ALU.mult)

        def gate(s):
            b, t = divmod(s, PACK)
            sig = tile([P, S], F32, "sig", bufs=PACK)
            cols = slice(P * t, P * t + P)
            for h in range(S // BANK):
                e = ring_bank([P, BANK], "e")
                js = slice(BANK * h, BANK * h + BANK)
                for a in range(2):
                    nc.tensor.matmul_mx(out=e[:], lhsT=w1_c[b, a][:, cols].bitcast(FP8X4), lhsT_scale=w1_s[b, a][:, cols],
                                        rhs=v_w[a][:, js].bitcast(FP8X4), rhs_scale=v_s[4 * a : P, js], start=(a == 0), stop=(a == 1))
                nc.scalar.activation(out=sig[:, js], in_=e[:], func=ACT.Sigmoid)
            nc.vector.tensor_tensor(out=a_t[s], in0=a_t[s], in1=sig[:], op=ALU.mult)

        z_lo = tile([P, PACK, S], BF16, "z_lo", tag="w1_raw00")
        z_hi = [tile([P, PACK, CHUNK], BF16, "z_hi%d" % c) for c in range(CHUNKS)]

        for s in range(PAGES):
            nc.vector.memset(pages[s][:], 0.0)
            place(s)
        for s in range(PACK):
            gate(s)
        for s in range(PACK):
            nc.vector.tensor_tensor(out=z_lo[:, s, :], in0=a_t[s], in1=pages[s][:], op=ALU.max)
            if s > 0:
                place(s - 1 + PAGES)
        quantise_w1(1)

        z_c = {}
        z_s = {}

        def quantise_z(b, c, src, copy):
            woven = tile([P, PACK * CHUNK], BF16, "woven", bufs=CHUNKS)
            copy(out=woven[:].rearrange("p (g l t) -> p g t l", l=4, t=PACK), in_=src.rearrange("p t (g l) -> p g t l", l=4))
            z_c[b, c] = tile([P, CHUNK], U32, "z_c%d%d" % (b, c))
            z_s[b, c] = tile([P, CHUNK], U8, "z_s%d%d" % (b, c))
            nc.vector.quantize_mx(out=z_c[b, c][:].bitcast(FP8X4), scales=z_s[b, c][:], in_=woven[:])

        w4_bf = tile([P, 2, PACK * N], BF16, "w4_bf")
        for b in range(2):
            nc.scalar.copy(out=w4_bf[:, b, :].rearrange("p (g l t) -> p g t l", l=4, t=PACK),
                           in_=w4_raw[:, b].rearrange("p t (g l) -> p g t l", l=4))
        w4_c = tile([P, 2 * N], U32, "w4_c")
        w4_s = tile([P, 2 * N], U8, "w4_s")
        nc.vector.quantize_mx(out=w4_c[:].bitcast(FP8X4), scales=w4_s[:], in_=w4_bf[:].rearrange("p b x -> p (b x)"))

        for s in range(PACK, SLICES):
            gate(s)
        for c in range(CHUNKS):
            quantise_z(0, c, z_lo[:, :, CHUNK * c : CHUNK * c + CHUNK], nc.scalar.copy)

        last = CHUNKS - 1
        for c in range(CHUNKS):
            js = slice(CHUNK * c, CHUNK * c + CHUNK)
            for t in range(PACK):
                s = PACK + t
                nc.vector.tensor_tensor(out=z_hi[c][:, t, :], in0=a_t[s][:, js], in1=pages[s % PAGES][:, js], op=ALU.max)
            quantise_z(1, c, z_hi[c][:], nc.vector.tensor_copy if c == last else nc.scalar.copy)
        for c in range(CHUNKS):
            acc = [ps.tile([P, CHUNK], F32, name="acc0", tag="arg"), ring_bank([P, CHUNK], "acc1")]
            for b in range(2):
                for n in range(2):
                    cols = slice(N * b + P * n, N * b + P * n + P)
                    nc.tensor.matmul_mx(out=acc[n][:], lhsT=w4_c[:, cols].bitcast(FP8X4), lhsT_scale=w4_s[:, cols],
                                        rhs=z_c[b, c][:].bitcast(FP8X4), rhs_scale=z_s[b, c][:], start=(b == 0), stop=(b == 1))
            res = tile([P, 2, CHUNK], F32, "res", bufs=CHUNKS)
            nc.scalar.copy(out=res[:, 0, :], in_=acc[0][:])
            if c == last:
                nc.vector.tensor_copy(out=res[:, 1, :], in_=acc[1][:])
            else:
                nc.scalar.copy(out=res[:, 1, :], in_=acc[1][:])
            nc.sync.dma_start(out=out[:, CHUNK * c : CHUNK * c + CHUNK].rearrange("(n p) j -> p n j", n=2), in_=res[:])
